import numpy as np
import ml_dtypes


def mxq(x, axis, fmt="e4m3"):
    dtype, down = {"e4m3": (ml_dtypes.float8_e4m3fn, 7), "e5m2": (ml_dtypes.float8_e5m2, 14)}[fmt]
    v = np.moveaxis(np.asarray(x, np.float32).astype(ml_dtypes.bfloat16).astype(np.float64), axis, -1)
    blocks = v.reshape(v.shape[:-1] + (-1, 32))
    amax = np.abs(blocks).max(-1, keepdims=True)
    byte = np.maximum(np.where(amax > 0, np.frexp(amax)[1] - 1 + 127, 0) - down, 1)
    scale = np.exp2(byte - 127.0)
    codes = (blocks / scale).astype(np.float32).astype(dtype).astype(np.float64)
    return np.moveaxis((codes * scale).reshape(v.shape), -1, axis)


WIDE = False


def mx_kscale(k):
    if not WIDE:
        return np.ones(k)
    levels = np.array([10, -10, 5, -5, 0])
    if k % 512:
        return np.exp2(np.random.permutation(np.resize(levels, k // 32))).repeat(32)
    a = np.empty((k // 512, 16))
    for p in range(k // 512):
        a[p, :8] = np.random.permutation(np.resize(levels, 8))
        for g in range(8):
            far = levels[np.abs(levels - a[p, g]) >= 10]
            a[p, g + 8] = far[np.random.randint(len(far))]
    return np.exp2(a.ravel()).repeat(32)


def f64(x):
    return np.asarray(x).astype(np.float64)


def striped(idx):
    return np.tile(np.asarray(idx).reshape(-1, 16).T, (8, 1)).astype(np.uint16)


def unstriped(offs):
    return offs[:16].T.reshape(-1).astype(np.int64)


E2M1 = np.array([0.0, 0.5, 1.0, 1.5, 2.0, 3.0, 4.0, 6.0, -0.0, -0.5, -1.0, -1.5, -2.0, -3.0, -4.0, -6.0])


def pack_weight(w, fmt):
    k, n = w.shape
    w = f64(np.asarray(w, np.float32).astype(ml_dtypes.bfloat16)).reshape(k // 32, 32, n)
    amax = np.abs(w).max(1)
    if fmt == "e4m3":
        byte = np.frexp(amax)[1] - 1 + 127 - 7
    else:
        mant, ex = np.frexp(amax / 6.0)
        byte = np.where(mant > 0.5, ex, ex - 1) + 127
    byte = np.clip(np.where(amax > 0, byte, 1), 1, 254)
    scaled = (w * np.exp2(127.0 - byte)[:, None, :]).reshape(k, n).astype(np.float32)
    by_word = np.ascontiguousarray(scaled.reshape(k // 512, 128, 4, n).transpose(0, 1, 3, 2))
    if fmt == "e4m3":
        words = by_word.astype(ml_dtypes.float8_e4m3fn).view(np.uint8)
    else:
        c = by_word.astype(ml_dtypes.float4_e2m1fn).view(np.uint8) & 0xF
        words = (c[..., 0::2] | (c[..., 1::2] << 4)).reshape(k // 512, 128, 2 * n)
    return np.ascontiguousarray(words), np.ascontiguousarray(byte.astype(np.uint8).reshape(k // 512, 16, n))


def unpack_weight(words, scales, fmt):
    g, _, n = scales.shape
    words = np.ascontiguousarray(words).reshape(g, 128, n, -1)
    if fmt == "e4m3":
        vals = words.view(ml_dtypes.float8_e4m3fn).astype(np.float64)
    else:
        nib = np.empty((g, 128, n, 4), np.uint8)
        nib[..., 0::2] = words & 0xF
        nib[..., 1::2] = words >> 4
        vals = E2M1[nib]
    vals = vals * np.repeat(np.exp2(scales.astype(np.float64) - 127.0), 8, axis=1)[..., None]
    return vals.transpose(0, 1, 3, 2).reshape(g * 512, n)


D, T, I, Q, J, U, M = 512, 2048, 512, 128, 512, 1024, 2048


def setup_inputs():
    n = np.random.standard_normal
    idx = np.random.permutation(T)[:I]
    idx2 = np.random.permutation(U)[:J]
    idx3 = np.random.permutation(M)[:I]
    fd = mx_kscale(D)
    fj = mx_kscale(J)
    tiesp = pack_weight(n((J, T)) * 0.08 / fj[:, None], "e2m1")
    return {
        "query": (n((D, Q)) * 1.0 / np.sqrt(D) * fd[:, None]).astype(np.float32),
        "hubs": (n((D, U)) / fd[:, None]).astype(np.float32),
        "hf": (np.random.uniform(0.5, 2.0, (J, 1)) * fj[:, None]).astype(np.float32),
        "ties_words": tiesp[0],
        "ties_scales": tiesp[1],
        "level": (np.random.uniform(0.05, 0.2, (Q, 1))).astype(np.float32),
        "old": (np.random.uniform(0.0, 2.0, (Q, M))).astype(np.float32),
        "fade": (np.random.uniform(0.3, 0.9, (Q, 1))).astype(np.float32),
        "offs": striped(idx),
        "offs2": striped(idx2),
        "offs3": striped(idx3),
    }


def reference(query, hubs, hf, ties_words, ties_scales, level, old, fade, offs, offs2, offs3):
    idx = unstriped(offs)
    idx2 = unstriped(offs2)
    idx3 = unstriped(offs3)
    tiesu = unpack_weight(ties_words, ties_scales, "e2m1")
    hubsidx2q = mxq(f64(hubs)[:, idx2], 0, "e4m3")
    queryq = mxq(f64(query), 0, "e4m3")
    hb = hubsidx2q.T @ queryq
    hp = np.maximum(hb, 0.0) * f64(hf)
    hpq = mxq(hp, 0, "e4m3")
    tiesidxg = tiesu[:, idx]
    s = hpq.T @ tiesidxg
    p = np.exp(s - np.max(s, axis=1, keepdims=True))
    r = p / np.sum(p, axis=1, keepdims=True)
    w = np.maximum(r - np.max(r, axis=1, keepdims=True) * f64(level), 0.0)
    ws = w * 256.0
    wf = np.zeros((Q, M))
    wf[:, idx3] = ws
    y = f64(old) * f64(fade) + wf
    return y

@@ -1,0 +1,209 @@
+from contextlib import ExitStack
+
+import concourse.mybir as mybir
+
+D, T, I, Q, J, U, M = 512, 2048, 512, 128, 512, 1024, 2048
+FLOPS = 2 * D * J * Q + 2 * J * Q * I
+
+F32 = mybir.dt.float32
+BF16 = mybir.dt.bfloat16
+I32 = mybir.dt.int32
+U32 = mybir.dt.uint32
+U16 = mybir.dt.uint16
+U8 = mybir.dt.uint8
+FP8X4 = mybir.dt.float8_e4m3fn_x4
+FP4X4 = mybir.dt.float4_e2m1fn_x4
+ALU = mybir.AluOpType
+ACT = mybir.ActivationFunctionType
+
+P = 128
+PACK = 4
+GROUP = 16
+VEC_SLOTS = 320
+OUT_CHUNKS = [256, 512, 512, 512, 256]
+
+
+def tile_attend_relayed_excess_counts_kernel(
+    tc, query, hubs, hf, ties_words, ties_scales, level, old, fade, offs, offs2, offs3, out
+):
+    nc = tc.nc
+    act_slots = J - VEC_SLOTS
+    vec_rows = VEC_SLOTS // PACK
+
+    with ExitStack() as ctx:
+        keep = ctx.enter_context(tc.tile_pool(name="keep", bufs=1))
+        wide = ctx.enter_context(tc.tile_pool(name="wide", bufs=PACK))
+        psum = ctx.enter_context(tc.psum_pool(name="psum", bufs=1))
+
+        hub_list = keep.tile([P, J // GROUP], U16, name="hub_list")
+        token_list = keep.tile([P, I // GROUP], U16, name="token_list")
+        column_list = keep.tile([P, I // GROUP], U16, name="column_list")
+
+        scale_pool = keep.tile([P, T], U8, name="scale_pool", align_bytes=64)
+        tie_scales = keep.tile([P, I], U8, name="tie_scales", align_bytes=64)
+        placed = keep.tile([P, M], F32, name="placed")
+        gain = keep.tile([P, I], F32, name="gain")
+        nc.vector.memset(scale_pool[:].bitcast(I32), 0)
+        nc.vector.memset(tie_scales[:].bitcast(I32), 0)
+        nc.vector.memset(placed[:], 0.0)
+        nc.vector.memset(gain[:], 256.0)
+
+        nc.sync.dma_start(out=hub_list[:], in_=offs2)
+        nc.sync.dma_start(out=token_list[:], in_=offs)
+        nc.scalar.dma_start(out=scale_pool[0:P:8, :].bitcast(I32), in_=ties_scales[0].bitcast(I32))
+
+        hub_rows = hubs.rearrange("(p t) u -> p t u", t=PACK)
+        planes = []
+        for t in range(PACK):
+            plane = wide.tile([P, U], F32, name="plane", tag="wide")
+            nc.sync.dma_start(out=plane[:], in_=hub_rows[:, t, :])
+            planes.append(plane)
+
+        query_raw = keep.tile([P, PACK, Q], F32, name="query_raw")
+        nc.sync.dma_start(out=query_raw[:], in_=query.rearrange("(p t) q -> p t q", t=PACK))
+        word_pool = keep.tile([P, T], U16, name="word_pool", align_bytes=64)
+        nc.sync.dma_start(out=word_pool[:].bitcast(I32), in_=ties_words[0].bitcast(I32))
+        nc.sync.dma_start(out=column_list[:], in_=offs3)
+
+        hub_factor = keep.tile([P, PACK], F32, name="hub_factor")
+        row_level = keep.tile([P, 1], F32, name="row_level")
+        row_fade = keep.tile([P, 1], F32, name="row_fade")
+        nc.sync.dma_start(out=hub_factor[:], in_=hf.rearrange("(p t) o -> p (t o)", t=PACK))
+        nc.sync.dma_start(out=row_level[:], in_=level)
+        nc.sync.dma_start(out=row_fade[:], in_=fade)
+
+        picked_scales = keep.tile([P, I], U8, name="picked_scales", align_bytes=64)
+        nc.vector.tensor_copy(out=picked_scales[:], in_=scale_pool[:].indirect(token_list[:]))
+        for f in range(PACK):
+            nc.sync.dma_start(
+                out=tie_scales[f:P:32, :].bitcast(I32),
+                in_=picked_scales[8 * f : P : 32, :].bitcast(I32),
+            )
+
+        hub_in = keep.tile([P, PACK, P, PACK], BF16, name="hub_in", align_bytes=64)
+        act_picked = keep.tile([P, PACK, act_slots], BF16, name="act_picked", align_bytes=64)
+        vec_list = hub_list[:, 0 : VEC_SLOTS // GROUP]
+        act_list = hub_list[:, VEC_SLOTS // GROUP : J // GROUP]
+        for t in range(PACK):
+            nc.vector.tensor_copy(
+                out=hub_in[:, :, 0:vec_rows, t].rearrange("p r m -> p m r"),
+                in_=planes[t][:].indirect(vec_list),
+            )
+            nc.scalar.activation(out=act_picked[:, t, :], in_=planes[t][:].indirect(act_list), func=ACT.Copy)
+        nc.scalar.copy(
+            out=hub_in[:, :, vec_rows:P, :].rearrange("p r (s e) t -> p s r e t", e=2),
+            in_=act_picked[:].rearrange("p t (s e r) -> p s r e t", e=2, r=PACK),
+        )
+
+        old_halves = []
+        for h in range(M // U):
+            old_half = wide.tile([P, U], F32, name="old_half", tag="wide")
+            nc.sync.dma_start(out=old_half[:], in_=old[:, h * U : (h + 1) * U])
+            old_halves.append(old_half)
+
+        query_in = keep.tile([P, Q, PACK], BF16, name="query_in", align_bytes=64)
+        nc.vector.tensor_copy(
+            out=query_in[:].rearrange("p (c e) t -> p c t e", e=4),
+            in_=query_raw[:].rearrange("p t (c e) -> p c t e", e=4),
+        )
+        query_codes = keep.tile([P, Q], U32, name="query_codes", align_bytes=64)
+        query_scales = keep.tile([P, Q], U8, name="query_scales", align_bytes=64)
+        nc.vector.quantize_mx(
+            out=query_codes[:].bitcast(FP8X4),
+            scales=query_scales[:],
+            in_=query_in[:].rearrange("p q t -> p (q t)"),
+        )
+
+        hub_codes = keep.tile([P, PACK, P], U32, name="hub_codes", align_bytes=64)
+        hub_scales = keep.tile([P, PACK, P], U8, name="hub_scales", align_bytes=64)
+        hub_sums = psum.tile([P, PACK, Q], F32, name="hub_sums")
+        for r in range(PACK):
+            nc.vector.quantize_mx(
+                out=hub_codes[:, r, :].bitcast(FP8X4),
+                scales=hub_scales[:, r, :],
+                in_=hub_in[:, r, :, :].rearrange("p m t -> p (m t)"),
+            )
+            nc.tensor.matmul_mx(
+                out=hub_sums[:, r, :],
+                lhsT=hub_codes[:, r, :].bitcast(FP8X4),
+                lhsT_scale=hub_scales[:, r, :],
+                rhs=query_codes[:].bitcast(FP8X4),
+                rhs_scale=query_scales[:],
+                start=True,
+                stop=True,
+            )
+
+        tie_words = keep.tile([P, I], U16, name="tie_words", align_bytes=64)
+        half = I // 2
+        nc.vector.tensor_copy(
+            out=tie_words[:, 0:half], in_=word_pool[:].indirect(token_list[:, 0 : half // GROUP])
+        )
+
+        relay_in = keep.tile([P, Q, PACK], BF16, name="relay_in", align_bytes=64)
+        nc.vector.scalar_tensor_tensor(
+            out=relay_in[:],
+            in0=hub_sums[:].rearrange("p r q -> p q r"),
+            scalar=0.0,
+            in1=hub_factor[:].unsqueeze(1).to_broadcast([P, Q, PACK]),
+            op0=ALU.max,
+            op1=ALU.mult,
+        )
+        nc.vector.tensor_copy(
+            out=tie_words[:, half:I], in_=word_pool[:].indirect(token_list[:, half // GROUP : I // GROUP])
+        )
+        relay_codes = keep.tile([P, Q], U32, name="relay_codes", align_bytes=64)
+        relay_scales = keep.tile([P, Q], U8, name="relay_scales", align_bytes=64)
+        nc.vector.quantize_mx(
+            out=relay_codes[:].bitcast(FP8X4),
+            scales=relay_scales[:],
+            in_=relay_in[:].rearrange("p q t -> p (q t)"),
+        )
+
+        scores = psum.tile([P, I], F32, name="scores")
+        nc.tensor.matmul_mx(
+            out=scores[:],
+            lhsT=relay_codes[:].bitcast(FP8X4),
+            lhsT_scale=relay_scales[:],
+            rhs=tie_words[:].bitcast(FP4X4),
+            rhs_scale=tie_scales[:],
+            start=True,
+            stop=True,
+        )
+
+        neg_max = keep.tile([P, 1], F32, name="neg_max")
+        nc.vector.tensor_reduce(out=neg_max[:], in_=scores[:], axis=mybir.AxisListType.X, op=ALU.max, negate=True)
+        shares = keep.tile([P, I], F32, name="shares")
+        row_sum = keep.tile([P, 1], F32, name="row_sum")
+        nc.scalar.activation(out=shares[:], in_=scores[:], func=ACT.Exp, bias=neg_max[:], accum_out=row_sum[:])
+        inv_sum = keep.tile([P, 1], F32, name="inv_sum")
+        nc.vector.reciprocal(out=inv_sum[:], in_=row_sum[:])
+        row_gain = keep.tile([P, I], F32, name="row_gain")
+        nc.scalar.activation(out=row_gain[:], in_=gain[:], func=ACT.Copy, scale=inv_sum[:])
+        excess = keep.tile([P, I], F32, name="excess")
+        nc.vector.tensor_scalar(
+            out=excess[:], in0=shares[:], scalar1=row_level[:], scalar2=0.0, op0=ALU.subtract, op1=ALU.max
+        )
+        nc.vector.tensor_tensor(
+            out=placed[:].indirect(column_list[:]), in0=excess[:], in1=row_gain[:], op=ALU.mult
+        )
+
+        start = 0
+        for c, width in enumerate(OUT_CHUNKS):
+            result = keep.tile([P, width], F32, name="result%d" % c)
+            pieces = []
+            lo = start
+            while lo < start + width:
+                hi = min(start + width, (lo // U + 1) * U)
+                pieces.append((lo, hi))
+                lo = hi
+            for lo, hi in pieces:
+                nc.vector.scalar_tensor_tensor(
+                    out=result[:, lo - start : hi - start],
+                    in0=old_halves[lo // U][:, lo % U : lo % U + hi - lo],
+                    scalar=row_fade[:],
+                    in1=placed[:, lo:hi],
+                    op0=ALU.mult,
+                    op1=ALU.add,
+                )
+            nc.sync.dma_start(out=out[:, start : start + width], in_=result[:])
+            start = start + width

@@ -19,7 +19,8 @@ ACT = mybir.ActivationFunctionType
 P = 128
 PACK = 4
 GROUP = 16
-VEC_SLOTS = 320
+VEC_SLOTS = 288
+FLOAT_TOP = 3.0e38
 OUT_CHUNKS = [256, 512, 512, 512, 256]
 
 
@@ -39,18 +40,17 @@ def tile_attend_relayed_excess_counts_kernel(
         token_list = keep.tile([P, I // GROUP], U16, name="token_list")
         column_list = keep.tile([P, I // GROUP], U16, name="column_list")
 
-        scale_pool = keep.tile([P, T], U8, name="scale_pool", align_bytes=64)
+        scale_pool = keep.tile([P, T // 4], I32, name="scale_pool", tag="early_late")
         tie_scales = keep.tile([P, I], U8, name="tie_scales", align_bytes=64)
         placed = keep.tile([P, M], F32, name="placed")
-        gain = keep.tile([P, I], F32, name="gain")
-        nc.vector.memset(scale_pool[:].bitcast(I32), 0)
+        gain = keep.tile([P, I // 2], F32, name="gain")
+        nc.vector.memset(scale_pool[0 : P - 16, :], 0)
         nc.vector.memset(tie_scales[:].bitcast(I32), 0)
         nc.vector.memset(placed[:], 0.0)
         nc.vector.memset(gain[:], 256.0)
 
-        nc.sync.dma_start(out=hub_list[:], in_=offs2)
         nc.sync.dma_start(out=token_list[:], in_=offs)
-        nc.scalar.dma_start(out=scale_pool[0:P:8, :].bitcast(I32), in_=ties_scales[0].bitcast(I32))
+        nc.scalar.dma_start(out=scale_pool[P - 16 : P, :], in_=ties_scales[0].bitcast(I32))
 
         hub_rows = hubs.rearrange("(p t) u -> p t u", t=PACK)
         planes = []
@@ -58,6 +58,8 @@ def tile_attend_relayed_excess_counts_kernel(
             plane = wide.tile([P, U], F32, name="plane", tag="wide")
             nc.sync.dma_start(out=plane[:], in_=hub_rows[:, t, :])
             planes.append(plane)
+            if t == 0:
+                nc.sync.dma_start(out=hub_list[:], in_=offs2)
 
         query_raw = keep.tile([P, PACK, Q], F32, name="query_raw")
         nc.sync.dma_start(out=query_raw[:], in_=query.rearrange("(p t) q -> p t q", t=PACK))
@@ -65,23 +67,25 @@ def tile_attend_relayed_excess_counts_kernel(
         nc.sync.dma_start(out=word_pool[:].bitcast(I32), in_=ties_words[0].bitcast(I32))
         nc.sync.dma_start(out=column_list[:], in_=offs3)
 
-        hub_factor = keep.tile([P, PACK], F32, name="hub_factor")
-        row_level = keep.tile([P, 1], F32, name="row_level")
-        row_fade = keep.tile([P, 1], F32, name="row_fade")
-        nc.sync.dma_start(out=hub_factor[:], in_=hf.rearrange("(p t) o -> p (t o)", t=PACK))
-        nc.sync.dma_start(out=row_level[:], in_=level)
-        nc.sync.dma_start(out=row_fade[:], in_=fade)
 
         picked_scales = keep.tile([P, I], U8, name="picked_scales", align_bytes=64)
-        nc.vector.tensor_copy(out=picked_scales[:], in_=scale_pool[:].indirect(token_list[:]))
+        nc.vector.tensor_copy(out=picked_scales[:], in_=scale_pool[:].bitcast(U8).indirect(token_list[:]))
         for f in range(PACK):
             nc.sync.dma_start(
                 out=tie_scales[f:P:32, :].bitcast(I32),
-                in_=picked_scales[8 * f : P : 32, :].bitcast(I32),
+                in_=picked_scales[P - 16 + f : P : 4, :].bitcast(I32),
             )
 
+        factors = keep.tile([P, 3, 8], F32, name="factors", tag="early_late")
+        hub_factor = factors[:, 0, 0:PACK]
+        row_level = factors[:, 1, 0:1]
+        row_fade = factors[:, 2, 0:1]
+        nc.sync.dma_start(out=hub_factor, in_=hf.rearrange("(p t) o -> p (t o)", t=PACK))
+        nc.sync.dma_start(out=row_level, in_=level)
+        nc.sync.dma_start(out=row_fade, in_=fade)
+
         hub_in = keep.tile([P, PACK, P, PACK], BF16, name="hub_in", align_bytes=64)
-        act_picked = keep.tile([P, PACK, act_slots], BF16, name="act_picked", align_bytes=64)
+        act_picked = keep.tile([P, PACK, act_slots], BF16, name="act_picked", tag="act_picked", align_bytes=64)
         vec_list = hub_list[:, 0 : VEC_SLOTS // GROUP]
         act_list = hub_list[:, VEC_SLOTS // GROUP : J // GROUP]
         for t in range(PACK):
@@ -90,10 +94,11 @@ def tile_attend_relayed_excess_counts_kernel(
                 in_=planes[t][:].indirect(vec_list),
             )
             nc.scalar.activation(out=act_picked[:, t, :], in_=planes[t][:].indirect(act_list), func=ACT.Copy)
-        nc.scalar.copy(
-            out=hub_in[:, :, vec_rows:P, :].rearrange("p r (s e) t -> p s r e t", e=2),
-            in_=act_picked[:].rearrange("p t (s e r) -> p s r e t", e=2, r=PACK),
-        )
+        for r0 in range(0, PACK, 2):
+            nc.scalar.copy(
+                out=hub_in[:, r0 : r0 + 2, vec_rows:P, :].rearrange("p r (s e) t -> p s r e t", e=2),
+                in_=act_picked[:].rearrange("p t (s e r) -> p s r e t", e=2, r=PACK)[:, :, r0 : r0 + 2, :, :],
+            )
 
         old_halves = []
         for h in range(M // U):
@@ -133,59 +138,90 @@ def tile_attend_relayed_excess_counts_kernel(
                 stop=True,
             )
 
-        tie_words = keep.tile([P, I], U16, name="tie_words", align_bytes=64)
         half = I // 2
-        nc.vector.tensor_copy(
-            out=tie_words[:, 0:half], in_=word_pool[:].indirect(token_list[:, 0 : half // GROUP])
-        )
+        half_cols = half // GROUP
+        tie_words_a = keep.tile([P, half], U16, name="tie_words_a", tag="act_picked", align_bytes=64)
+        nc.vector.tensor_copy(out=tie_words_a[:], in_=word_pool[:].indirect(token_list[:, 0:half_cols]))
 
-        relay_in = keep.tile([P, Q, PACK], BF16, name="relay_in", align_bytes=64)
-        nc.vector.scalar_tensor_tensor(
-            out=relay_in[:],
-            in0=hub_sums[:].rearrange("p r q -> p q r"),
-            scalar=0.0,
-            in1=hub_factor[:].unsqueeze(1).to_broadcast([P, Q, PACK]),
-            op0=ALU.max,
-            op1=ALU.mult,
-        )
-        nc.vector.tensor_copy(
-            out=tie_words[:, half:I], in_=word_pool[:].indirect(token_list[:, half // GROUP : I // GROUP])
-        )
+        rows = Q // 2
+        relay_ins = []
+        for h in range(2):
+            relay_in = keep.tile([P, rows, PACK], BF16, name="relay_in", tag="relay_in%d" % h, align_bytes=64)
+            nc.vector.scalar_tensor_tensor(
+                out=relay_in[:],
+                in0=hub_sums[:, :, h * rows : (h + 1) * rows].rearrange("p r q -> p q r"),
+                scalar=0.0,
+                in1=hub_factor.unsqueeze(1).to_broadcast([P, rows, PACK]),
+                op0=ALU.max,
+                op1=ALU.mult,
+            )
+            relay_ins.append(relay_in)
         relay_codes = keep.tile([P, Q], U32, name="relay_codes", align_bytes=64)
         relay_scales = keep.tile([P, Q], U8, name="relay_scales", align_bytes=64)
-        nc.vector.quantize_mx(
-            out=relay_codes[:].bitcast(FP8X4),
-            scales=relay_scales[:],
-            in_=relay_in[:].rearrange("p q t -> p (q t)"),
-        )
+        for h in range(2):
+            nc.vector.quantize_mx(
+                out=relay_codes[:, h * rows : (h + 1) * rows].bitcast(FP8X4),
+                scales=relay_scales[:, h * rows : (h + 1) * rows],
+                in_=relay_ins[h][:].rearrange("p q t -> p (q t)"),
+            )
+        tie_words_b = keep.tile([P, half], U16, name="tie_words_b", tag="relay_in0", align_bytes=64)
+        nc.vector.tensor_copy(out=tie_words_b[:], in_=word_pool[:].indirect(token_list[:, half_cols : 2 * half_cols]))
 
-        scores = psum.tile([P, I], F32, name="scores")
-        nc.tensor.matmul_mx(
-            out=scores[:],
-            lhsT=relay_codes[:].bitcast(FP8X4),
-            lhsT_scale=relay_scales[:],
-            rhs=tie_words[:].bitcast(FP4X4),
-            rhs_scale=tie_scales[:],
-            start=True,
-            stop=True,
-        )
+        neg_scores = keep.tile([P, I], F32, name="neg_scores")
+        neg_max = FLOAT_TOP
+        for h, tie_words in enumerate((tie_words_a, tie_words_b)):
+            scores = psum.tile([P, half], F32, name="scores%d" % h)
+            nc.tensor.matmul_mx(
+                out=scores[:],
+                lhsT=relay_codes[:].bitcast(FP8X4),
+                lhsT_scale=relay_scales[:],
+                rhs=tie_words[:].bitcast(FP4X4),
+                rhs_scale=tie_scales[:, h * half : (h + 1) * half],
+                start=True,
+                stop=True,
+            )
+            least = keep.tile([P, 1], F32, name="least%d" % h)
+            nc.vector.tensor_scalar(
+                out=neg_scores[:, h * half : (h + 1) * half],
+                in0=scores[:],
+                scalar1=-1.0,
+                scalar2=neg_max,
+                op0=ALU.mult,
+                op1=ALU.min,
+                accum_out=least[:],
+            )
+            neg_max = least[:]
 
-        neg_max = keep.tile([P, 1], F32, name="neg_max")
-        nc.vector.tensor_reduce(out=neg_max[:], in_=scores[:], axis=mybir.AxisListType.X, op=ALU.max, negate=True)
         shares = keep.tile([P, I], F32, name="shares")
         row_sum = keep.tile([P, 1], F32, name="row_sum")
-        nc.scalar.activation(out=shares[:], in_=scores[:], func=ACT.Exp, bias=neg_max[:], accum_out=row_sum[:])
+        nc.scalar.activation(
+            out=shares[:], in_=neg_scores[:], func=ACT.Exp, bias=neg_max, scale=-1.0, accum_out=row_sum[:]
+        )
         inv_sum = keep.tile([P, 1], F32, name="inv_sum")
         nc.vector.reciprocal(out=inv_sum[:], in_=row_sum[:])
-        row_gain = keep.tile([P, I], F32, name="row_gain")
-        nc.scalar.activation(out=row_gain[:], in_=gain[:], func=ACT.Copy, scale=inv_sum[:])
         excess = keep.tile([P, I], F32, name="excess")
-        nc.vector.tensor_scalar(
-            out=excess[:], in0=shares[:], scalar1=row_level[:], scalar2=0.0, op0=ALU.subtract, op1=ALU.max
-        )
-        nc.vector.tensor_tensor(
-            out=placed[:].indirect(column_list[:]), in0=excess[:], in1=row_gain[:], op=ALU.mult
-        )
+        row_gain = keep.tile([P, half], F32, name="row_gain")
+
+        def cut(h):
+            nc.vector.tensor_scalar(
+                out=excess[:, h * half : (h + 1) * half],
+                in0=shares[:, h * half : (h + 1) * half],
+                scalar1=row_level,
+                scalar2=0.0,
+                op0=ALU.subtract,
+                op1=ALU.max,
+            )
+
+        cut(0)
+        nc.vector.tensor_scalar_mul(out=row_gain[:], in0=gain[:], scalar1=inv_sum[:])
+        cut(1)
+        for h in range(2):
+            nc.vector.tensor_tensor(
+                out=placed[:].indirect(column_list[:, h * half_cols : (h + 1) * half_cols]),
+                in0=excess[:, h * half : (h + 1) * half],
+                in1=row_gain[:],
+                op=ALU.mult,
+            )
 
         start = 0
         for c, width in enumerate(OUT_CHUNKS):
@@ -200,7 +236,7 @@ def tile_attend_relayed_excess_counts_kernel(
                 nc.vector.scalar_tensor_tensor(
                     out=result[:, lo - start : hi - start],
                     in0=old_halves[lo // U][:, lo % U : lo % U + hi - lo],
-                    scalar=row_fade[:],
+                    scalar=row_fade,
                     in1=placed[:, lo:hi],
                     op0=ALU.mult,
                     op1=ALU.add,

@@ -19,7 +19,7 @@ ACT = mybir.ActivationFunctionType
 P = 128
 PACK = 4
 GROUP = 16
-VEC_SLOTS = 288
+VEC_SLOTS = 320
 FLOAT_TOP = 3.0e38
 OUT_CHUNKS = [256, 512, 512, 512, 256]
 
@@ -44,13 +44,17 @@ def tile_attend_relayed_excess_counts_kernel(
         tie_scales = keep.tile([P, I], U8, name="tie_scales", align_bytes=64)
         placed = keep.tile([P, M], F32, name="placed")
         gain = keep.tile([P, I // 2], F32, name="gain")
+        unit = keep.tile([P, 1], F32, name="unit")
+        nc.vector.memset(unit[:], 1.0)
+        nc.scalar.activation(out=gain[:], in_=unit[:].to_broadcast([P, I // 2]), func=ACT.Copy, scale=256.0)
         nc.vector.memset(scale_pool[0 : P - 16, :], 0)
         nc.vector.memset(tie_scales[:].bitcast(I32), 0)
         nc.vector.memset(placed[:], 0.0)
-        nc.vector.memset(gain[:], 256.0)
 
         nc.sync.dma_start(out=token_list[:], in_=offs)
         nc.scalar.dma_start(out=scale_pool[P - 16 : P, :], in_=ties_scales[0].bitcast(I32))
+        hub_factor = keep.tile([P, PACK], F32, name="hub_factor")
+        nc.scalar.dma_start(out=hub_factor[:], in_=hf.rearrange("(p t) o -> p (t o)", t=PACK))
 
         hub_rows = hubs.rearrange("(p t) u -> p t u", t=PACK)
         planes = []
@@ -76,11 +80,9 @@ def tile_attend_relayed_excess_counts_kernel(
                 in_=picked_scales[P - 16 + f : P : 4, :].bitcast(I32),
             )
 
-        factors = keep.tile([P, 3, 8], F32, name="factors", tag="early_late")
-        hub_factor = factors[:, 0, 0:PACK]
-        row_level = factors[:, 1, 0:1]
-        row_fade = factors[:, 2, 0:1]
-        nc.sync.dma_start(out=hub_factor, in_=hf.rearrange("(p t) o -> p (t o)", t=PACK))
+        factors = keep.tile([P, 2, 8], F32, name="factors", tag="early_late")
+        row_level = factors[:, 0, 0:1]
+        row_fade = factors[:, 1, 0:1]
         nc.sync.dma_start(out=row_level, in_=level)
         nc.sync.dma_start(out=row_fade, in_=fade)
 
@@ -151,7 +153,7 @@ def tile_attend_relayed_excess_counts_kernel(
                 out=relay_in[:],
                 in0=hub_sums[:, :, h * rows : (h + 1) * rows].rearrange("p r q -> p q r"),
                 scalar=0.0,
-                in1=hub_factor.unsqueeze(1).to_broadcast([P, rows, PACK]),
+                in1=hub_factor[:].unsqueeze(1).to_broadcast([P, rows, PACK]),
                 op0=ALU.max,
                 op1=ALU.mult,
             )

@@ -19,7 +19,7 @@ ACT = mybir.ActivationFunctionType
 P = 128
 PACK = 4
 GROUP = 16
-VEC_SLOTS = 320
+VEC_SLOTS = 352
 FLOAT_TOP = 3.0e38
 OUT_CHUNKS = [256, 512, 512, 512, 256]
 
@@ -43,17 +43,17 @@ def tile_attend_relayed_excess_counts_kernel(
         scale_pool = keep.tile([P, T // 4], I32, name="scale_pool", tag="early_late")
         tie_scales = keep.tile([P, I], U8, name="tie_scales", align_bytes=64)
         placed = keep.tile([P, M], F32, name="placed")
-        gain = keep.tile([P, I // 2], F32, name="gain")
+        gain = keep.tile([P, I], F32, name="gain")
         unit = keep.tile([P, 1], F32, name="unit")
         nc.vector.memset(unit[:], 1.0)
-        nc.scalar.activation(out=gain[:], in_=unit[:].to_broadcast([P, I // 2]), func=ACT.Copy, scale=256.0)
+        nc.scalar.activation(out=gain[:], in_=unit[:].to_broadcast([P, I]), func=ACT.Copy, scale=256.0)
         nc.vector.memset(scale_pool[0 : P - 16, :], 0)
         nc.vector.memset(tie_scales[:].bitcast(I32), 0)
         nc.vector.memset(placed[:], 0.0)
 
         nc.sync.dma_start(out=token_list[:], in_=offs)
         nc.scalar.dma_start(out=scale_pool[P - 16 : P, :], in_=ties_scales[0].bitcast(I32))
-        hub_factor = keep.tile([P, PACK], F32, name="hub_factor")
+        hub_factor = keep.tile([P, PACK], F32, name="hub_factor", tag="hub_factor", align_bytes=64)
         nc.scalar.dma_start(out=hub_factor[:], in_=hf.rearrange("(p t) o -> p (t o)", t=PACK))
 
         hub_rows = hubs.rearrange("(p t) u -> p t u", t=PACK)
@@ -115,12 +115,6 @@ def tile_attend_relayed_excess_counts_kernel(
         )
         query_codes = keep.tile([P, Q], U32, name="query_codes", align_bytes=64)
         query_scales = keep.tile([P, Q], U8, name="query_scales", align_bytes=64)
-        nc.vector.quantize_mx(
-            out=query_codes[:].bitcast(FP8X4),
-            scales=query_scales[:],
-            in_=query_in[:].rearrange("p q t -> p (q t)"),
-        )
-
         hub_codes = keep.tile([P, PACK, P], U32, name="hub_codes", align_bytes=64)
         hub_scales = keep.tile([P, PACK, P], U8, name="hub_scales", align_bytes=64)
         hub_sums = psum.tile([P, PACK, Q], F32, name="hub_sums")
@@ -130,6 +124,12 @@ def tile_attend_relayed_excess_counts_kernel(
                 scales=hub_scales[:, r, :],
                 in_=hub_in[:, r, :, :].rearrange("p m t -> p (m t)"),
             )
+            if r == 0:
+                nc.vector.quantize_mx(
+                    out=query_codes[:].bitcast(FP8X4),
+                    scales=query_scales[:],
+                    in_=query_in[:].rearrange("p q t -> p (q t)"),
+                )
             nc.tensor.matmul_mx(
                 out=hub_sums[:, r, :],
                 lhsT=hub_codes[:, r, :].bitcast(FP8X4),
@@ -142,31 +142,25 @@ def tile_attend_relayed_excess_counts_kernel(
 
         half = I // 2
         half_cols = half // GROUP
+        relay_in = keep.tile([P, Q, PACK], BF16, name="relay_in", align_bytes=64)
+        nc.vector.scalar_tensor_tensor(
+            out=relay_in[:],
+            in0=hub_sums[:].rearrange("p r q -> p q r"),
+            scalar=0.0,
+            in1=hub_factor[:].unsqueeze(1).to_broadcast([P, Q, PACK]),
+            op0=ALU.max,
+            op1=ALU.mult,
+        )
         tie_words_a = keep.tile([P, half], U16, name="tie_words_a", tag="act_picked", align_bytes=64)
         nc.vector.tensor_copy(out=tie_words_a[:], in_=word_pool[:].indirect(token_list[:, 0:half_cols]))
-
-        rows = Q // 2
-        relay_ins = []
-        for h in range(2):
-            relay_in = keep.tile([P, rows, PACK], BF16, name="relay_in", tag="relay_in%d" % h, align_bytes=64)
-            nc.vector.scalar_tensor_tensor(
-                out=relay_in[:],
-                in0=hub_sums[:, :, h * rows : (h + 1) * rows].rearrange("p r q -> p q r"),
-                scalar=0.0,
-                in1=hub_factor[:].unsqueeze(1).to_broadcast([P, rows, PACK]),
-                op0=ALU.max,
-                op1=ALU.mult,
-            )
-            relay_ins.append(relay_in)
         relay_codes = keep.tile([P, Q], U32, name="relay_codes", align_bytes=64)
         relay_scales = keep.tile([P, Q], U8, name="relay_scales", align_bytes=64)
-        for h in range(2):
-            nc.vector.quantize_mx(
-                out=relay_codes[:, h * rows : (h + 1) * rows].bitcast(FP8X4),
-                scales=relay_scales[:, h * rows : (h + 1) * rows],
-                in_=relay_ins[h][:].rearrange("p q t -> p (q t)"),
-            )
-        tie_words_b = keep.tile([P, half], U16, name="tie_words_b", tag="relay_in0", align_bytes=64)
+        nc.vector.quantize_mx(
+            out=relay_codes[:].bitcast(FP8X4),
+            scales=relay_scales[:],
+            in_=relay_in[:].rearrange("p q t -> p (q t)"),
+        )
+        tie_words_b = keep.tile([P, half], U16, name="tie_words_b", tag="hub_factor", align_bytes=64)
         nc.vector.tensor_copy(out=tie_words_b[:], in_=word_pool[:].indirect(token_list[:, half_cols : 2 * half_cols]))
 
         neg_scores = keep.tile([P, I], F32, name="neg_scores")
@@ -202,28 +196,13 @@ def tile_attend_relayed_excess_counts_kernel(
         inv_sum = keep.tile([P, 1], F32, name="inv_sum")
         nc.vector.reciprocal(out=inv_sum[:], in_=row_sum[:])
         excess = keep.tile([P, I], F32, name="excess")
-        row_gain = keep.tile([P, half], F32, name="row_gain")
-
-        def cut(h):
-            nc.vector.tensor_scalar(
-                out=excess[:, h * half : (h + 1) * half],
-                in0=shares[:, h * half : (h + 1) * half],
-                scalar1=row_level,
-                scalar2=0.0,
-                op0=ALU.subtract,
-                op1=ALU.max,
-            )
-
-        cut(0)
-        nc.vector.tensor_scalar_mul(out=row_gain[:], in0=gain[:], scalar1=inv_sum[:])
-        cut(1)
-        for h in range(2):
-            nc.vector.tensor_tensor(
-                out=placed[:].indirect(column_list[:, h * half_cols : (h + 1) * half_cols]),
-                in0=excess[:, h * half : (h + 1) * half],
-                in1=row_gain[:],
-                op=ALU.mult,
-            )
+        row_gain = keep.tile([P, I], F32, name="row_gain")
+        nc.vector.tensor_scalar(
+            out=excess[:], in0=shares[:], scalar1=row_level, scalar2=0.0, op0=ALU.subtract, op1=ALU.max
+        )
+        nc.vector.tensor_scalar_mul(out=row_gain[:, 0:half], in0=gain[:, 0:half], scalar1=inv_sum[:])
+        nc.scalar.activation(out=row_gain[:, half:I], in_=gain[:, half:I], func=ACT.Copy, scale=inv_sum[:])
+        nc.vector.tensor_tensor(out=placed[:].indirect(column_list[:]), in0=excess[:], in1=row_gain[:], op=ALU.mult)
 
         start = 0
         for c, width in enumerate(OUT_CHUNKS):

from contextlib import ExitStack

import concourse.mybir as mybir

D, T, I, Q, J, U, M = 512, 2048, 512, 128, 512, 1024, 2048
FLOPS = 2 * D * J * Q + 2 * J * Q * I

F32 = mybir.dt.float32
BF16 = mybir.dt.bfloat16
I32 = mybir.dt.int32
U32 = mybir.dt.uint32
U16 = mybir.dt.uint16
U8 = mybir.dt.uint8
FP8X4 = mybir.dt.float8_e4m3fn_x4
FP4X4 = mybir.dt.float4_e2m1fn_x4
ALU = mybir.AluOpType
ACT = mybir.ActivationFunctionType

P = 128
PACK = 4
GROUP = 16
VEC_SLOTS = 352
FLOAT_TOP = 3.0e38
OUT_CHUNKS = [256, 512, 512, 512, 256]


def tile_attend_relayed_excess_counts_kernel(
    tc, query, hubs, hf, ties_words, ties_scales, level, old, fade, offs, offs2, offs3, out
):
    nc = tc.nc
    act_slots = J - VEC_SLOTS
    vec_rows = VEC_SLOTS // PACK

    with ExitStack() as ctx:
        keep = ctx.enter_context(tc.tile_pool(name="keep", bufs=1))
        wide = ctx.enter_context(tc.tile_pool(name="wide", bufs=PACK))
        psum = ctx.enter_context(tc.psum_pool(name="psum", bufs=1))

        hub_list = keep.tile([P, J // GROUP], U16, name="hub_list")
        token_list = keep.tile([P, I // GROUP], U16, name="token_list")
        column_list = keep.tile([P, I // GROUP], U16, name="column_list")

        scale_pool = keep.tile([P, T // 4], I32, name="scale_pool", tag="early_late")
        tie_scales = keep.tile([P, I], U8, name="tie_scales", align_bytes=64)
        placed = keep.tile([P, M], F32, name="placed")
        gain = keep.tile([P, I], F32, name="gain")
        unit = keep.tile([P, 1], F32, name="unit")
        nc.vector.memset(unit[:], 1.0)
        nc.scalar.activation(out=gain[:], in_=unit[:].to_broadcast([P, I]), func=ACT.Copy, scale=256.0)
        nc.vector.memset(scale_pool[0 : P - 16, :], 0)
        nc.vector.memset(tie_scales[:].bitcast(I32), 0)
        nc.vector.memset(placed[:], 0.0)

        nc.sync.dma_start(out=token_list[:], in_=offs)
        nc.scalar.dma_start(out=scale_pool[P - 16 : P, :], in_=ties_scales[0].bitcast(I32))
        hub_factor = keep.tile([P, PACK], F32, name="hub_factor", tag="hub_factor", align_bytes=64)
        nc.scalar.dma_start(out=hub_factor[:], in_=hf.rearrange("(p t) o -> p (t o)", t=PACK))

        hub_rows = hubs.rearrange("(p t) u -> p t u", t=PACK)
        planes = []
        for t in range(PACK):
            plane = wide.tile([P, U], F32, name="plane", tag="wide")
            nc.sync.dma_start(out=plane[:], in_=hub_rows[:, t, :])
            planes.append(plane)
            if t == 0:
                nc.sync.dma_start(out=hub_list[:], in_=offs2)

        query_raw = keep.tile([P, PACK, Q], F32, name="query_raw")
        nc.sync.dma_start(out=query_raw[:], in_=query.rearrange("(p t) q -> p t q", t=PACK))
        word_pool = keep.tile([P, T], U16, name="word_pool", align_bytes=64)
        nc.sync.dma_start(out=word_pool[:].bitcast(I32), in_=ties_words[0].bitcast(I32))
        nc.sync.dma_start(out=column_list[:], in_=offs3)


        picked_scales = keep.tile([P, I], U8, name="picked_scales", align_bytes=64)
        nc.vector.tensor_copy(out=picked_scales[:], in_=scale_pool[:].bitcast(U8).indirect(token_list[:]))
        for f in range(PACK):
            nc.sync.dma_start(
                out=tie_scales[f:P:32, :].bitcast(I32),
                in_=picked_scales[P - 16 + f : P : 4, :].bitcast(I32),
            )

        factors = keep.tile([P, 2, 8], F32, name="factors", tag="early_late")
        row_level = factors[:, 0, 0:1]
        row_fade = factors[:, 1, 0:1]
        nc.sync.dma_start(out=row_level, in_=level)
        nc.sync.dma_start(out=row_fade, in_=fade)

        hub_in = keep.tile([P, PACK, P, PACK], BF16, name="hub_in", align_bytes=64)
        act_picked = keep.tile([P, PACK, act_slots], BF16, name="act_picked", tag="act_picked", align_bytes=64)
        vec_list = hub_list[:, 0 : VEC_SLOTS // GROUP]
        act_list = hub_list[:, VEC_SLOTS // GROUP : J // GROUP]
        for t in range(PACK):
            nc.vector.tensor_copy(
                out=hub_in[:, :, 0:vec_rows, t].rearrange("p r m -> p m r"),
                in_=planes[t][:].indirect(vec_list),
            )
            nc.scalar.activation(out=act_picked[:, t, :], in_=planes[t][:].indirect(act_list), func=ACT.Copy)
        for r0 in range(0, PACK, 2):
            nc.scalar.copy(
                out=hub_in[:, r0 : r0 + 2, vec_rows:P, :].rearrange("p r (s e) t -> p s r e t", e=2),
                in_=act_picked[:].rearrange("p t (s e r) -> p s r e t", e=2, r=PACK)[:, :, r0 : r0 + 2, :, :],
            )

        old_halves = []
        for h in range(M // U):
            old_half = wide.tile([P, U], F32, name="old_half", tag="wide")
            nc.sync.dma_start(out=old_half[:], in_=old[:, h * U : (h + 1) * U])
            old_halves.append(old_half)

        query_in = keep.tile([P, Q, PACK], BF16, name="query_in", align_bytes=64)
        nc.vector.tensor_copy(
            out=query_in[:].rearrange("p (c e) t -> p c t e", e=4),
            in_=query_raw[:].rearrange("p t (c e) -> p c t e", e=4),
        )
        query_codes = keep.tile([P, Q], U32, name="query_codes", align_bytes=64)
        query_scales = keep.tile([P, Q], U8, name="query_scales", align_bytes=64)
        hub_codes = keep.tile([P, PACK, P], U32, name="hub_codes", align_bytes=64)
        hub_scales = keep.tile([P, PACK, P], U8, name="hub_scales", align_bytes=64)
        hub_sums = psum.tile([P, PACK, Q], F32, name="hub_sums")
        for r in range(PACK):
            nc.vector.quantize_mx(
                out=hub_codes[:, r, :].bitcast(FP8X4),
                scales=hub_scales[:, r, :],
                in_=hub_in[:, r, :, :].rearrange("p m t -> p (m t)"),
            )
            if r == 0:
                nc.vector.quantize_mx(
                    out=query_codes[:].bitcast(FP8X4),
                    scales=query_scales[:],
                    in_=query_in[:].rearrange("p q t -> p (q t)"),
                )
            nc.tensor.matmul_mx(
                out=hub_sums[:, r, :],
                lhsT=hub_codes[:, r, :].bitcast(FP8X4),
                lhsT_scale=hub_scales[:, r, :],
                rhs=query_codes[:].bitcast(FP8X4),
                rhs_scale=query_scales[:],
                start=True,
                stop=True,
            )

        half = I // 2
        half_cols = half // GROUP
        relay_in = keep.tile([P, Q, PACK], BF16, name="relay_in", align_bytes=64)
        nc.vector.scalar_tensor_tensor(
            out=relay_in[:],
            in0=hub_sums[:].rearrange("p r q -> p q r"),
            scalar=0.0,
            in1=hub_factor[:].unsqueeze(1).to_broadcast([P, Q, PACK]),
            op0=ALU.max,
            op1=ALU.mult,
        )
        tie_words_a = keep.tile([P, half], U16, name="tie_words_a", tag="act_picked", align_bytes=64)
        nc.vector.tensor_copy(out=tie_words_a[:], in_=word_pool[:].indirect(token_list[:, 0:half_cols]))
        relay_codes = keep.tile([P, Q], U32, name="relay_codes", align_bytes=64)
        relay_scales = keep.tile([P, Q], U8, name="relay_scales", align_bytes=64)
        nc.vector.quantize_mx(
            out=relay_codes[:].bitcast(FP8X4),
            scales=relay_scales[:],
            in_=relay_in[:].rearrange("p q t -> p (q t)"),
        )
        tie_words_b = keep.tile([P, half], U16, name="tie_words_b", tag="hub_factor", align_bytes=64)
        nc.vector.tensor_copy(out=tie_words_b[:], in_=word_pool[:].indirect(token_list[:, half_cols : 2 * half_cols]))

        neg_scores = keep.tile([P, I], F32, name="neg_scores")
        neg_max = FLOAT_TOP
        for h, tie_words in enumerate((tie_words_a, tie_words_b)):
            scores = psum.tile([P, half], F32, name="scores%d" % h)
            nc.tensor.matmul_mx(
                out=scores[:],
                lhsT=relay_codes[:].bitcast(FP8X4),
                lhsT_scale=relay_scales[:],
                rhs=tie_words[:].bitcast(FP4X4),
                rhs_scale=tie_scales[:, h * half : (h + 1) * half],
                start=True,
                stop=True,
            )
            least = keep.tile([P, 1], F32, name="least%d" % h)
            nc.vector.tensor_scalar(
                out=neg_scores[:, h * half : (h + 1) * half],
                in0=scores[:],
                scalar1=-1.0,
                scalar2=neg_max,
                op0=ALU.mult,
                op1=ALU.min,
                accum_out=least[:],
            )
            neg_max = least[:]

        shares = keep.tile([P, I], F32, name="shares")
        row_sum = keep.tile([P, 1], F32, name="row_sum")
        nc.scalar.activation(
            out=shares[:], in_=neg_scores[:], func=ACT.Exp, bias=neg_max, scale=-1.0, accum_out=row_sum[:]
        )
        inv_sum = keep.tile([P, 1], F32, name="inv_sum")
        nc.vector.reciprocal(out=inv_sum[:], in_=row_sum[:])
        excess = keep.tile([P, I], F32, name="excess")
        row_gain = keep.tile([P, I], F32, name="row_gain")
        nc.vector.tensor_scalar(
            out=excess[:], in0=shares[:], scalar1=row_level, scalar2=0.0, op0=ALU.subtract, op1=ALU.max
        )
        nc.vector.tensor_scalar_mul(out=row_gain[:, 0:half], in0=gain[:, 0:half], scalar1=inv_sum[:])
        nc.scalar.activation(out=row_gain[:, half:I], in_=gain[:, half:I], func=ACT.Copy, scale=inv_sum[:])
        nc.vector.tensor_tensor(out=placed[:].indirect(column_list[:]), in0=excess[:], in1=row_gain[:], op=ALU.mult)

        start = 0
        for c, width in enumerate(OUT_CHUNKS):
            result = keep.tile([P, width], F32, name="result%d" % c)
            pieces = []
            lo = start
            while lo < start + width:
                hi = min(start + width, (lo // U + 1) * U)
                pieces.append((lo, hi))
                lo = hi
            for lo, hi in pieces:
                nc.vector.scalar_tensor_tensor(
                    out=result[:, lo - start : hi - start],
                    in0=old_halves[lo // U][:, lo % U : lo % U + hi - lo],
                    scalar=row_fade,
                    in1=placed[:, lo:hi],
                    op0=ALU.mult,
                    op1=ALU.add,
                )
            nc.sync.dma_start(out=out[:, start : start + width], in_=result[:])
            start = start + width
